import numpy as np
CORES = [7,15,23,31,39,47,55,63,71,79,87,95,103,111,119,127]
N = 16
ROOT = 15
def setup_inputs(rng):
    return {"x": rng.standard_normal((N, 128, 4096), dtype=np.float32)}
def reference(x):
    return {"y": np.broadcast_to(x[ROOT], x.shape)}

@@ -1,0 +1,216 @@
+import concourse.bass as bass
+
+MODE = "fan"
+NCH = 64
+WAVES = [8, 8, 8, 8]
+ROOT = 127
+NCOL = 4096 // NCH
+RPS = 128 // NCH
+
+SCRATCH = {"buf": ("dram", [NCH, 128, NCOL], "float32")}
+SEMAPHORES = ["st", "sent",
+              "l0", "l1", "l2", "l3", "l4", "l5", "l6", "l7",
+              "a0", "a1", "a2", "a3", "a4", "a5", "a6", "a7",
+              "f0", "f1", "f2", "f3", "f4", "f5", "f6", "f7",
+              "f8", "f9", "f10", "f11", "f12", "f13", "f14", "f15"]
+
+
+def emask(first, n):
+    return ((1 << n) - 1) << first
+
+
+def with_masks(transfers):
+    per = 8
+    while per * len(transfers) > 8:
+        per //= 2
+    return [(s, d, k, emask(i * per, per)) for i, (s, d, k) in enumerate(transfers)]
+
+
+def totals(root_calls, duties):
+    inc = {}
+    calls = list(root_calls)
+    for c in sorted(duties):
+        calls += [call for key, call in duties[c]]
+    for call in calls:
+        for s, dests, key, mask in call:
+            for d in dests:
+                inc[(d, key)] = inc.get((d, key), 0) + bin(mask).count("1")
+    return inc
+
+
+def build_fan():
+    duties = {}
+    root_calls = []
+    groups = []
+    waves = []
+    ctr = {}
+    used = {}
+
+    def relay_for(die, par):
+        j = ctr.get((die, par), 0)
+        ctr[(die, par)] = j + 1
+        chip = 2 * (j % 8) if par == 0 else 2 * ((j + 2 * die) % 7) + 1
+        k = used.get((chip, die), 0)
+        used[(chip, die)] = k + 1
+        return chip * 8 + (6 if die == 0 else (3, 2)[k % 2])
+
+    def fan_out(relay, slot, grp):
+        chip = relay // 8
+        order = [(chip + i) % 16 for i in range(1, 16)]
+        same = [c * 8 + 7 for c in order if c != 15 and c % 2 == chip % 2]
+        other = [c * 8 + 7 for c in order if c != 15 and c % 2 != chip % 2]
+        if len(same) <= len(other):
+            same = [chip * 8 + 7] + same
+        else:
+            other = [chip * 8 + 7] + other
+        key = ("a", len(duties.setdefault(relay, [])))
+        duties[relay].append((key, with_masks([(slot, same, ("f", grp)), (slot, other, ("f", grp))])))
+        return key
+
+    slot = 0
+    for m in WAVES:
+        per = 8 // m
+        call = []
+        waves.append((slot, 2 * m))
+        grp = len(groups)
+        groups.append((slot, m, [("f", grp)]))
+        for t in range(m):
+            relay = relay_for(0, t % 2)
+            call.append((slot, [relay], fan_out(relay, slot, grp), emask(t * per, per)))
+            slot += 1
+        grp = len(groups)
+        groups.append((slot, m, [("f", grp)]))
+        hand = {}
+        for t in range(m):
+            relay = relay_for(1, t % 2)
+            helper = (122 if t % 2 == 0 else 120) + (t // 2) % 2
+            hand.setdefault(helper, []).append((slot, [relay], fan_out(relay, slot, grp)))
+            key = ("a", len(duties.get(helper, [])))
+            call.append((slot, [helper], key, emask(8 + t * per, per)))
+            slot += 1
+        for helper in sorted(hand):
+            key = ("a", len(duties.get(helper, [])))
+            duties.setdefault(helper, []).append((key, with_masks(hand[helper])))
+        root_calls.append(call)
+    return root_calls, duties, groups, waves, totals(root_calls, duties)
+
+
+def build_mate():
+    duties = {}
+    root_calls = []
+    groups = []
+    waves = []
+    ctr = {}
+    turn = [0]
+    fwd_core = (6, 3)
+
+    def relay_to_plane(die, par, slot, w, via15):
+        j = ctr.get((die, par), 0)
+        ctr[(die, par)] = j + 1
+        chip = 2 * (j % 7) + par
+        relay = chip * 8 + ((4, 5) if die == 0 else (0, 1))[(j // 7) % 2]
+        order = [(chip + 2 * i) % 16 for i in range(1, 9)]
+        dests = [c * 8 + fwd_core[die] for c in order if c != 15 or via15]
+        key = ("a", len(duties.setdefault(relay, [])))
+        duties[relay].append((key, with_masks([(slot, dests, ("a", w))])))
+        return relay, key
+
+    slot = 0
+    for w, m in enumerate(WAVES):
+        per = 8 // m
+        h = m // 2
+        call = []
+        hand = {}
+        waves.append((slot, 2 * m))
+        for die in (0, 1):
+            groups.append((slot, m, [("f", 4 * w + 2 * die), ("f", 4 * w + 2 * die + 1)]))
+            for par in (0, 1):
+                fkey = ("f", 4 * w + 2 * die + par)
+                via15 = par == 1 and (w + die) % 2 == 0
+                extra = None
+                if par == 1 and not via15:
+                    extra = 2 * (turn[0] % 7) + 1
+                    turn[0] += 3
+                first = slot
+                for t in range(h):
+                    relay, key = relay_to_plane(die, par, slot, w, via15)
+                    e = (par * h + t) * per
+                    if die == 0:
+                        call.append((slot, [relay], key, emask(e, per)))
+                    else:
+                        helper = 122 if par == 0 else 120 + t % 2
+                        hand.setdefault(helper, []).append((slot, [relay], key))
+                        call.append((slot, [helper], ("a", w), emask(8 + e, per)))
+                    slot += 1
+                for chip in range(par, 16, 2):
+                    if chip == 15 and not via15:
+                        continue
+                    dests = [c * 8 + 7 for c in (chip, chip ^ 1) if c != 15]
+                    if chip == extra:
+                        dests.append(119)
+                    duties.setdefault(chip * 8 + fwd_core[die], []).append(
+                        (("a", w), with_masks([(s, dests, fkey) for s in range(first, first + h)])))
+        for helper in sorted(hand):
+            duties.setdefault(helper, []).append((("a", w), with_masks(hand[helper])))
+        root_calls.append(call)
+    return root_calls, duties, groups, waves, totals(root_calls, duties)
+
+
+def rank_program(g, core, T, topo):
+    root_calls, duties, groups, waves, inc = build_fan() if MODE == "fan" else build_mate()
+    asem = [T.sem.a0, T.sem.a1, T.sem.a2, T.sem.a3, T.sem.a4, T.sem.a5, T.sem.a6, T.sem.a7]
+    fsem = [T.sem.f0, T.sem.f1, T.sem.f2, T.sem.f3, T.sem.f4, T.sem.f5, T.sem.f6, T.sem.f7,
+            T.sem.f8, T.sem.f9, T.sem.f10, T.sem.f11, T.sem.f12, T.sem.f13, T.sem.f14, T.sem.f15]
+
+    def sem(key):
+        return asem[key[1]] if key[0] == "a" else fsem[key[1]]
+
+    def fused(call):
+        tl = []
+        left = 0
+        for s, dests, key, mask in call:
+            ids = []
+            for d in dests:
+                rid, pid, se = topo.addr(d)
+                ids.append(bass.DstId(rid=rid, pnc=pid))
+            tl.append(bass.RemoteDMATransfer(dst_ids=ids, dma_engine_mask=mask, remote_sem=sem(key),
+                                             srcs=[T.buf[s]], dsts=[T.buf[s] for d in dests]))
+            left += bin(mask).count("1")
+        g.remote_dma_fused(tl, local_sem=T.sem.sent)
+        return left
+
+    if core == ROOT:
+        lsem = [T.sem.l0, T.sem.l1, T.sem.l2, T.sem.l3, T.sem.l4, T.sem.l5, T.sem.l6, T.sem.l7]
+
+        def load(w):
+            s0, n = waves[w]
+            g.dma_start(T.buf[s0:s0 + n], T.x[s0 * RPS:(s0 + n) * RPS, :]).then_inc(lsem[w], 16)
+        load(0)
+        if len(waves) > 1:
+            load(1)
+        left = 0
+        for w, call in enumerate(root_calls):
+            g.wait_ge(lsem[w], 16)
+            left += fused(call)
+            if w + 2 < len(waves):
+                load(w + 2)
+        g.dma_start(T.y[:, :], T.x[:, :]).then_inc(T.sem.st, 16)
+        g.wait_ge(T.sem.sent, left)
+        g.wait_ge(T.sem.st, 16)
+        return
+
+    if core in duties:
+        left = 0
+        for key, call in duties[core]:
+            g.wait_ge(sem(key), inc[(core, key)])
+            left += fused(call)
+        g.wait_ge(T.sem.sent, left)
+        return
+
+    if T.rank_of(core) is None:
+        return
+    for s0, n, keys in groups:
+        for key in keys:
+            g.wait_ge(sem(key), inc[(core, key)])
+        g.dma_start(T.y[s0 * RPS:(s0 + n) * RPS, :], T.buf[s0:s0 + n]).then_inc(T.sem.st, 16)
+    g.wait_ge(T.sem.st, 16 * len(groups))

@@ -1,15 +1,23 @@
 import concourse.bass as bass
 
-MODE = "fan"
-NCH = 64
-WAVES = [8, 8, 8, 8]
+SEGS = [(4, [(8, 8)]), (4, [(8, 8)]), (4, [(8, 8)]), (4, [(8, 8)])]
+PRE = 2
+SPLIT = 8
+YJOIN = ()
 ROOT = 127
-NCOL = 4096 // NCH
-RPS = 128 // NCH
 
-SCRATCH = {"buf": ("dram", [NCH, 128, NCOL], "float32")}
+
+def seg_shape(i):
+    if i >= len(SEGS):
+        return [1, 128, 1]
+    return [sum(a + b for a, b in SEGS[i][1]), 128, 16 * SEGS[i][0]]
+
+
+SCRATCH = {"b0": ("dram", seg_shape(0), "float32"), "b1": ("dram", seg_shape(1), "float32"),
+           "b2": ("dram", seg_shape(2), "float32"), "b3": ("dram", seg_shape(3), "float32"),
+           "b4": ("dram", seg_shape(4), "float32"), "b5": ("dram", seg_shape(5), "float32")}
 SEMAPHORES = ["st", "sent",
-              "l0", "l1", "l2", "l3", "l4", "l5", "l6", "l7",
+              "l0", "l1", "l2", "l3", "l4", "l5",
               "a0", "a1", "a2", "a3", "a4", "a5", "a6", "a7",
               "f0", "f1", "f2", "f3", "f4", "f5", "f6", "f7",
               "f8", "f9", "f10", "f11", "f12", "f13", "f14", "f15"]
@@ -28,7 +36,7 @@ def with_masks(transfers):
 
 def totals(root_calls, duties):
     inc = {}
-    calls = list(root_calls)
+    calls = [call for seg, call in root_calls]
     for c in sorted(duties):
         calls += [call for key, call in duties[c]]
     for call in calls:
@@ -38,11 +46,11 @@ def totals(root_calls, duties):
     return inc
 
 
-def build_fan():
+def build_plan():
     duties = {}
     root_calls = []
     groups = []
-    waves = []
+    loads = []
     ctr = {}
     used = {}
 
@@ -54,7 +62,7 @@ def build_fan():
         used[(chip, die)] = k + 1
         return chip * 8 + (6 if die == 0 else (3, 2)[k % 2])
 
-    def fan_out(relay, slot, grp):
+    def fan_out(relay, ref, fkey):
         chip = relay // 8
         order = [(chip + i) % 16 for i in range(1, 16)]
         same = [c * 8 + 7 for c in order if c != 15 and c % 2 == chip % 2]
@@ -63,101 +71,48 @@ def build_fan():
             same = [chip * 8 + 7] + same
         else:
             other = [chip * 8 + 7] + other
+        q = SPLIT // 2
+        lists = [same[i::q] for i in range(q)] + [other[i::q] for i in range(q)]
         key = ("a", len(duties.setdefault(relay, [])))
-        duties[relay].append((key, with_masks([(slot, same, ("f", grp)), (slot, other, ("f", grp))])))
+        duties[relay].append((key, with_masks([(ref, ds, fkey) for ds in lists])))
         return key
 
-    slot = 0
-    for m in WAVES:
-        per = 8 // m
-        call = []
-        waves.append((slot, 2 * m))
-        grp = len(groups)
-        groups.append((slot, m, [("f", grp)]))
-        for t in range(m):
-            relay = relay_for(0, t % 2)
-            call.append((slot, [relay], fan_out(relay, slot, grp), emask(t * per, per)))
-            slot += 1
-        grp = len(groups)
-        groups.append((slot, m, [("f", grp)]))
-        hand = {}
-        for t in range(m):
-            relay = relay_for(1, t % 2)
-            helper = (122 if t % 2 == 0 else 120) + (t // 2) % 2
-            hand.setdefault(helper, []).append((slot, [relay], fan_out(relay, slot, grp)))
-            key = ("a", len(duties.get(helper, [])))
-            call.append((slot, [helper], key, emask(8 + t * per, per)))
-            slot += 1
-        for helper in sorted(hand):
-            key = ("a", len(duties.get(helper, [])))
-            duties.setdefault(helper, []).append((key, with_masks(hand[helper])))
-        root_calls.append(call)
-    return root_calls, duties, groups, waves, totals(root_calls, duties)
-
-
-def build_mate():
-    duties = {}
-    root_calls = []
-    groups = []
-    waves = []
-    ctr = {}
-    turn = [0]
-    fwd_core = (6, 3)
-
-    def relay_to_plane(die, par, slot, w, via15):
-        j = ctr.get((die, par), 0)
-        ctr[(die, par)] = j + 1
-        chip = 2 * (j % 7) + par
-        relay = chip * 8 + ((4, 5) if die == 0 else (0, 1))[(j // 7) % 2]
-        order = [(chip + 2 * i) % 16 for i in range(1, 9)]
-        dests = [c * 8 + fwd_core[die] for c in order if c != 15 or via15]
-        key = ("a", len(duties.setdefault(relay, [])))
-        duties[relay].append((key, with_masks([(slot, dests, ("a", w))])))
-        return relay, key
-
-    slot = 0
-    for w, m in enumerate(WAVES):
-        per = 8 // m
-        h = m // 2
-        call = []
-        hand = {}
-        waves.append((slot, 2 * m))
-        for die in (0, 1):
-            groups.append((slot, m, [("f", 4 * w + 2 * die), ("f", 4 * w + 2 * die + 1)]))
-            for par in (0, 1):
-                fkey = ("f", 4 * w + 2 * die + par)
-                via15 = par == 1 and (w + die) % 2 == 0
-                extra = None
-                if par == 1 and not via15:
-                    extra = 2 * (turn[0] % 7) + 1
-                    turn[0] += 3
-                first = slot
-                for t in range(h):
-                    relay, key = relay_to_plane(die, par, slot, w, via15)
-                    e = (par * h + t) * per
-                    if die == 0:
-                        call.append((slot, [relay], key, emask(e, per)))
+    half = 0
+    for seg, (size, wv) in enumerate(SEGS):
+        slot = 0
+        start = half
+        for md, mh in wv:
+            call = []
+            hand = {}
+            for part, m in ((0, md), (1, mh)):
+                if m == 0:
+                    continue
+                fkey = ("f", len(groups))
+                groups.append((seg, slot, m, half // 2, m * size // 2, fkey))
+                per = 8 // m
+                for t in range(m):
+                    ref = (seg, slot)
+                    if part == 0:
+                        relay = relay_for(0 if mh else (t // 2) % 2, t % 2)
+                        call.append((ref, [relay], fan_out(relay, ref, fkey), emask(t * per, per)))
                     else:
-                        helper = 122 if par == 0 else 120 + t % 2
-                        hand.setdefault(helper, []).append((slot, [relay], key))
-                        call.append((slot, [helper], ("a", w), emask(8 + e, per)))
+                        relay = relay_for(1, t % 2)
+                        helper = (122 if t % 2 == 0 else 120) + (t // 2) % 2
+                        hand.setdefault(helper, []).append((ref, [relay], fan_out(relay, ref, fkey)))
+                        call.append((ref, [helper], ("a", len(duties.get(helper, []))), emask(8 + t * per, per)))
                     slot += 1
-                for chip in range(par, 16, 2):
-                    if chip == 15 and not via15:
-                        continue
-                    dests = [c * 8 + 7 for c in (chip, chip ^ 1) if c != 15]
-                    if chip == extra:
-                        dests.append(119)
-                    duties.setdefault(chip * 8 + fwd_core[die], []).append(
-                        (("a", w), with_masks([(s, dests, fkey) for s in range(first, first + h)])))
-        for helper in sorted(hand):
-            duties.setdefault(helper, []).append((("a", w), with_masks(hand[helper])))
-        root_calls.append(call)
-    return root_calls, duties, groups, waves, totals(root_calls, duties)
+                    half += size
+            for helper in sorted(hand):
+                key = ("a", len(duties.get(helper, [])))
+                duties.setdefault(helper, []).append((key, with_masks(hand[helper])))
+            root_calls.append((seg, call))
+        loads.append((start // 2, (half - start) // 2))
+    return root_calls, duties, groups, loads, totals(root_calls, duties)
 
 
 def rank_program(g, core, T, topo):
-    root_calls, duties, groups, waves, inc = build_fan() if MODE == "fan" else build_mate()
+    root_calls, duties, groups, loads, inc = build_plan()
+    bufs = [T.b0, T.b1, T.b2, T.b3, T.b4, T.b5]
     asem = [T.sem.a0, T.sem.a1, T.sem.a2, T.sem.a3, T.sem.a4, T.sem.a5, T.sem.a6, T.sem.a7]
     fsem = [T.sem.f0, T.sem.f1, T.sem.f2, T.sem.f3, T.sem.f4, T.sem.f5, T.sem.f6, T.sem.f7,
             T.sem.f8, T.sem.f9, T.sem.f10, T.sem.f11, T.sem.f12, T.sem.f13, T.sem.f14, T.sem.f15]
@@ -168,32 +123,37 @@ def rank_program(g, core, T, topo):
     def fused(call):
         tl = []
         left = 0
-        for s, dests, key, mask in call:
+        for (seg, s), dests, key, mask in call:
             ids = []
             for d in dests:
                 rid, pid, se = topo.addr(d)
                 ids.append(bass.DstId(rid=rid, pnc=pid))
             tl.append(bass.RemoteDMATransfer(dst_ids=ids, dma_engine_mask=mask, remote_sem=sem(key),
-                                             srcs=[T.buf[s]], dsts=[T.buf[s] for d in dests]))
+                                             srcs=[bufs[seg][s]], dsts=[bufs[seg][s] for d in dests]))
             left += bin(mask).count("1")
         g.remote_dma_fused(tl, local_sem=T.sem.sent)
         return left
 
     if core == ROOT:
-        lsem = [T.sem.l0, T.sem.l1, T.sem.l2, T.sem.l3, T.sem.l4, T.sem.l5, T.sem.l6, T.sem.l7]
+        lsem = [T.sem.l0, T.sem.l1, T.sem.l2, T.sem.l3, T.sem.l4, T.sem.l5]
 
-        def load(w):
-            s0, n = waves[w]
-            g.dma_start(T.buf[s0:s0 + n], T.x[s0 * RPS:(s0 + n) * RPS, :]).then_inc(lsem[w], 16)
-        load(0)
-        if len(waves) > 1:
-            load(1)
+        def load(i):
+            r0, n = loads[i]
+            g.dma_start(bufs[i][:], T.x[r0:r0 + n, :]).then_inc(lsem[i], 16)
+        nxt = 0
+        while nxt < min(PRE, len(loads)):
+            load(nxt)
+            nxt += 1
         left = 0
-        for w, call in enumerate(root_calls):
-            g.wait_ge(lsem[w], 16)
+        ready = -1
+        for seg, call in root_calls:
+            if seg > ready:
+                g.wait_ge(lsem[seg], 16)
+                ready = seg
             left += fused(call)
-            if w + 2 < len(waves):
-                load(w + 2)
+            if nxt < len(loads):
+                load(nxt)
+                nxt += 1
         g.dma_start(T.y[:, :], T.x[:, :]).then_inc(T.sem.st, 16)
         g.wait_ge(T.sem.sent, left)
         g.wait_ge(T.sem.st, 16)
@@ -209,8 +169,17 @@ def rank_program(g, core, T, topo):
 
     if T.rank_of(core) is None:
         return
-    for s0, n, keys in groups:
-        for key in keys:
-            g.wait_ge(sem(key), inc[(core, key)])
-        g.dma_start(T.y[s0 * RPS:(s0 + n) * RPS, :], T.buf[s0:s0 + n]).then_inc(T.sem.st, 16)
-    g.wait_ge(T.sem.st, 16 * len(groups))
+    copies = []
+    for i, grp in enumerate(groups):
+        if copies and i in YJOIN:
+            copies[-1].append(grp)
+        else:
+            copies.append([grp])
+    for cp in copies:
+        for grp in cp:
+            g.wait_ge(sem(grp[5]), inc[(core, grp[5])])
+        seg, s0, r0 = cp[0][0], cp[0][1], cp[0][3]
+        n = sum(grp[2] for grp in cp)
+        nr = sum(grp[4] for grp in cp)
+        g.dma_start(T.y[r0:r0 + nr, :], bufs[seg][s0:s0 + n]).then_inc(T.sem.st, 16)
+    g.wait_ge(T.sem.st, 16 * len(copies))

@@ -1,26 +1,22 @@
 import concourse.bass as bass
 
-SEGS = [(4, [(8, 8)]), (4, [(8, 8)]), (4, [(8, 8)]), (4, [(8, 8)])]
+SIZE = 4
+WAVES = [(8, 8), (8, 8), (8, 8), (8, 8)]
 PRE = 2
 SPLIT = 8
-YJOIN = ()
 ROOT = 127
 
 
-def seg_shape(i):
-    if i >= len(SEGS):
-        return [1, 128, 1]
-    return [sum(a + b for a, b in SEGS[i][1]), 128, 16 * SEGS[i][0]]
+def wave_shape(i):
+    return [WAVES[i][0] + WAVES[i][1], 128, 16 * SIZE]
 
 
-SCRATCH = {"b0": ("dram", seg_shape(0), "float32"), "b1": ("dram", seg_shape(1), "float32"),
-           "b2": ("dram", seg_shape(2), "float32"), "b3": ("dram", seg_shape(3), "float32"),
-           "b4": ("dram", seg_shape(4), "float32"), "b5": ("dram", seg_shape(5), "float32")}
+SCRATCH = {"b0": ("dram", wave_shape(0), "float32"), "b1": ("dram", wave_shape(1), "float32"),
+           "b2": ("dram", wave_shape(2), "float32"), "b3": ("dram", wave_shape(3), "float32")}
 SEMAPHORES = ["st", "sent",
-              "l0", "l1", "l2", "l3", "l4", "l5",
-              "a0", "a1", "a2", "a3", "a4", "a5", "a6", "a7",
-              "f0", "f1", "f2", "f3", "f4", "f5", "f6", "f7",
-              "f8", "f9", "f10", "f11", "f12", "f13", "f14", "f15"]
+              "l0", "l1", "l2", "l3",
+              "a0", "a1", "a2", "a3",
+              "f0", "f1", "f2", "f3", "f4", "f5", "f6", "f7"]
 
 
 def emask(first, n):
@@ -36,7 +32,7 @@ def with_masks(transfers):
 
 def totals(root_calls, duties):
     inc = {}
-    calls = [call for seg, call in root_calls]
+    calls = list(root_calls)
     for c in sorted(duties):
         calls += [call for key, call in duties[c]]
     for call in calls:
@@ -78,44 +74,40 @@ def build_plan():
         return key
 
     half = 0
-    for seg, (size, wv) in enumerate(SEGS):
+    for w, (md, mh) in enumerate(WAVES):
         slot = 0
         start = half
-        for md, mh in wv:
-            call = []
-            hand = {}
-            for part, m in ((0, md), (1, mh)):
-                if m == 0:
-                    continue
-                fkey = ("f", len(groups))
-                groups.append((seg, slot, m, half // 2, m * size // 2, fkey))
-                per = 8 // m
-                for t in range(m):
-                    ref = (seg, slot)
-                    if part == 0:
-                        relay = relay_for(0 if mh else (t // 2) % 2, t % 2)
-                        call.append((ref, [relay], fan_out(relay, ref, fkey), emask(t * per, per)))
-                    else:
-                        relay = relay_for(1, t % 2)
-                        helper = (122 if t % 2 == 0 else 120) + (t // 2) % 2
-                        hand.setdefault(helper, []).append((ref, [relay], fan_out(relay, ref, fkey)))
-                        call.append((ref, [helper], ("a", len(duties.get(helper, []))), emask(8 + t * per, per)))
-                    slot += 1
-                    half += size
-            for helper in sorted(hand):
-                key = ("a", len(duties.get(helper, [])))
-                duties.setdefault(helper, []).append((key, with_masks(hand[helper])))
-            root_calls.append((seg, call))
+        call = []
+        hand = {}
+        for part, m in ((0, md), (1, mh)):
+            fkey = ("f", len(groups))
+            groups.append((w, slot, m, half // 2, m * SIZE // 2, fkey))
+            per = 8 // m
+            for t in range(m):
+                ref = (w, slot)
+                relay = relay_for(part, t % 2)
+                key = fan_out(relay, ref, fkey)
+                if part == 0:
+                    call.append((ref, [relay], key, emask(t * per, per)))
+                else:
+                    helper = (122 if t % 2 == 0 else 120) + (t // 2) % 2
+                    hand.setdefault(helper, []).append((ref, [relay], key))
+                    call.append((ref, [helper], ("a", len(duties.get(helper, []))), emask(8 + t * per, per)))
+                slot += 1
+                half += SIZE
+        for helper in sorted(hand):
+            key = ("a", len(duties.get(helper, [])))
+            duties.setdefault(helper, []).append((key, with_masks(hand[helper])))
+        root_calls.append(call)
         loads.append((start // 2, (half - start) // 2))
     return root_calls, duties, groups, loads, totals(root_calls, duties)
 
 
 def rank_program(g, core, T, topo):
     root_calls, duties, groups, loads, inc = build_plan()
-    bufs = [T.b0, T.b1, T.b2, T.b3, T.b4, T.b5]
-    asem = [T.sem.a0, T.sem.a1, T.sem.a2, T.sem.a3, T.sem.a4, T.sem.a5, T.sem.a6, T.sem.a7]
-    fsem = [T.sem.f0, T.sem.f1, T.sem.f2, T.sem.f3, T.sem.f4, T.sem.f5, T.sem.f6, T.sem.f7,
-            T.sem.f8, T.sem.f9, T.sem.f10, T.sem.f11, T.sem.f12, T.sem.f13, T.sem.f14, T.sem.f15]
+    bufs = [T.b0, T.b1, T.b2, T.b3]
+    asem = [T.sem.a0, T.sem.a1, T.sem.a2, T.sem.a3]
+    fsem = [T.sem.f0, T.sem.f1, T.sem.f2, T.sem.f3, T.sem.f4, T.sem.f5, T.sem.f6, T.sem.f7]
 
     def sem(key):
         return asem[key[1]] if key[0] == "a" else fsem[key[1]]
@@ -123,19 +115,19 @@ def rank_program(g, core, T, topo):
     def fused(call):
         tl = []
         left = 0
-        for (seg, s), dests, key, mask in call:
+        for (w, s), dests, key, mask in call:
             ids = []
             for d in dests:
                 rid, pid, se = topo.addr(d)
                 ids.append(bass.DstId(rid=rid, pnc=pid))
             tl.append(bass.RemoteDMATransfer(dst_ids=ids, dma_engine_mask=mask, remote_sem=sem(key),
-                                             srcs=[bufs[seg][s]], dsts=[bufs[seg][s] for d in dests]))
+                                             srcs=[bufs[w][s]], dsts=[bufs[w][s] for d in dests]))
             left += bin(mask).count("1")
         g.remote_dma_fused(tl, local_sem=T.sem.sent)
         return left
 
     if core == ROOT:
-        lsem = [T.sem.l0, T.sem.l1, T.sem.l2, T.sem.l3, T.sem.l4, T.sem.l5]
+        lsem = [T.sem.l0, T.sem.l1, T.sem.l2, T.sem.l3]
 
         def load(i):
             r0, n = loads[i]
@@ -145,11 +137,8 @@ def rank_program(g, core, T, topo):
             load(nxt)
             nxt += 1
         left = 0
-        ready = -1
-        for seg, call in root_calls:
-            if seg > ready:
-                g.wait_ge(lsem[seg], 16)
-                ready = seg
+        for w, call in enumerate(root_calls):
+            g.wait_ge(lsem[w], 16)
             left += fused(call)
             if nxt < len(loads):
                 load(nxt)
@@ -169,17 +158,7 @@ def rank_program(g, core, T, topo):
 
     if T.rank_of(core) is None:
         return
-    copies = []
-    for i, grp in enumerate(groups):
-        if copies and i in YJOIN:
-            copies[-1].append(grp)
-        else:
-            copies.append([grp])
-    for cp in copies:
-        for grp in cp:
-            g.wait_ge(sem(grp[5]), inc[(core, grp[5])])
-        seg, s0, r0 = cp[0][0], cp[0][1], cp[0][3]
-        n = sum(grp[2] for grp in cp)
-        nr = sum(grp[4] for grp in cp)
-        g.dma_start(T.y[r0:r0 + nr, :], bufs[seg][s0:s0 + n]).then_inc(T.sem.st, 16)
-    g.wait_ge(T.sem.st, 16 * len(copies))
+    for w, s0, n, r0, nr, key in groups:
+        g.wait_ge(sem(key), inc[(core, key)])
+        g.dma_start(T.y[r0:r0 + nr, :], bufs[w][s0:s0 + n]).then_inc(T.sem.st, 16)
+    g.wait_ge(T.sem.st, 16 * len(groups))

import concourse.bass as bass

SIZE = 4
WAVES = [(8, 8), (8, 8), (8, 8), (8, 8)]
PRE = 2
SPLIT = 8
ROOT = 127


def wave_shape(i):
    return [WAVES[i][0] + WAVES[i][1], 128, 16 * SIZE]


SCRATCH = {"b0": ("dram", wave_shape(0), "float32"), "b1": ("dram", wave_shape(1), "float32"),
           "b2": ("dram", wave_shape(2), "float32"), "b3": ("dram", wave_shape(3), "float32")}
SEMAPHORES = ["st", "sent",
              "l0", "l1", "l2", "l3",
              "a0", "a1", "a2", "a3",
              "f0", "f1", "f2", "f3", "f4", "f5", "f6", "f7"]


def emask(first, n):
    return ((1 << n) - 1) << first


def with_masks(transfers):
    per = 8
    while per * len(transfers) > 8:
        per //= 2
    return [(s, d, k, emask(i * per, per)) for i, (s, d, k) in enumerate(transfers)]


def totals(root_calls, duties):
    inc = {}
    calls = list(root_calls)
    for c in sorted(duties):
        calls += [call for key, call in duties[c]]
    for call in calls:
        for s, dests, key, mask in call:
            for d in dests:
                inc[(d, key)] = inc.get((d, key), 0) + bin(mask).count("1")
    return inc


def build_plan():
    duties = {}
    root_calls = []
    groups = []
    loads = []
    ctr = {}
    used = {}

    def relay_for(die, par):
        j = ctr.get((die, par), 0)
        ctr[(die, par)] = j + 1
        chip = 2 * (j % 8) if par == 0 else 2 * ((j + 2 * die) % 7) + 1
        k = used.get((chip, die), 0)
        used[(chip, die)] = k + 1
        return chip * 8 + (6 if die == 0 else (3, 2)[k % 2])

    def fan_out(relay, ref, fkey):
        chip = relay // 8
        order = [(chip + i) % 16 for i in range(1, 16)]
        same = [c * 8 + 7 for c in order if c != 15 and c % 2 == chip % 2]
        other = [c * 8 + 7 for c in order if c != 15 and c % 2 != chip % 2]
        if len(same) <= len(other):
            same = [chip * 8 + 7] + same
        else:
            other = [chip * 8 + 7] + other
        q = SPLIT // 2
        lists = [same[i::q] for i in range(q)] + [other[i::q] for i in range(q)]
        key = ("a", len(duties.setdefault(relay, [])))
        duties[relay].append((key, with_masks([(ref, ds, fkey) for ds in lists])))
        return key

    half = 0
    for w, (md, mh) in enumerate(WAVES):
        slot = 0
        start = half
        call = []
        hand = {}
        for part, m in ((0, md), (1, mh)):
            fkey = ("f", len(groups))
            groups.append((w, slot, m, half // 2, m * SIZE // 2, fkey))
            per = 8 // m
            for t in range(m):
                ref = (w, slot)
                relay = relay_for(part, t % 2)
                key = fan_out(relay, ref, fkey)
                if part == 0:
                    call.append((ref, [relay], key, emask(t * per, per)))
                else:
                    helper = (122 if t % 2 == 0 else 120) + (t // 2) % 2
                    hand.setdefault(helper, []).append((ref, [relay], key))
                    call.append((ref, [helper], ("a", len(duties.get(helper, []))), emask(8 + t * per, per)))
                slot += 1
                half += SIZE
        for helper in sorted(hand):
            key = ("a", len(duties.get(helper, [])))
            duties.setdefault(helper, []).append((key, with_masks(hand[helper])))
        root_calls.append(call)
        loads.append((start // 2, (half - start) // 2))
    return root_calls, duties, groups, loads, totals(root_calls, duties)


def rank_program(g, core, T, topo):
    root_calls, duties, groups, loads, inc = build_plan()
    bufs = [T.b0, T.b1, T.b2, T.b3]
    asem = [T.sem.a0, T.sem.a1, T.sem.a2, T.sem.a3]
    fsem = [T.sem.f0, T.sem.f1, T.sem.f2, T.sem.f3, T.sem.f4, T.sem.f5, T.sem.f6, T.sem.f7]

    def sem(key):
        return asem[key[1]] if key[0] == "a" else fsem[key[1]]

    def fused(call):
        tl = []
        left = 0
        for (w, s), dests, key, mask in call:
            ids = []
            for d in dests:
                rid, pid, se = topo.addr(d)
                ids.append(bass.DstId(rid=rid, pnc=pid))
            tl.append(bass.RemoteDMATransfer(dst_ids=ids, dma_engine_mask=mask, remote_sem=sem(key),
                                             srcs=[bufs[w][s]], dsts=[bufs[w][s] for d in dests]))
            left += bin(mask).count("1")
        g.remote_dma_fused(tl, local_sem=T.sem.sent)
        return left

    if core == ROOT:
        lsem = [T.sem.l0, T.sem.l1, T.sem.l2, T.sem.l3]

        def load(i):
            r0, n = loads[i]
            g.dma_start(bufs[i][:], T.x[r0:r0 + n, :]).then_inc(lsem[i], 16)
        nxt = 0
        while nxt < min(PRE, len(loads)):
            load(nxt)
            nxt += 1
        left = 0
        for w, call in enumerate(root_calls):
            g.wait_ge(lsem[w], 16)
            left += fused(call)
            if nxt < len(loads):
                load(nxt)
                nxt += 1
        g.dma_start(T.y[:, :], T.x[:, :]).then_inc(T.sem.st, 16)
        g.wait_ge(T.sem.sent, left)
        g.wait_ge(T.sem.st, 16)
        return

    if core in duties:
        left = 0
        for key, call in duties[core]:
            g.wait_ge(sem(key), inc[(core, key)])
            left += fused(call)
        g.wait_ge(T.sem.sent, left)
        return

    if T.rank_of(core) is None:
        return
    for w, s0, n, r0, nr, key in groups:
        g.wait_ge(sem(key), inc[(core, key)])
        g.dma_start(T.y[r0:r0 + nr, :], bufs[w][s0:s0 + n]).then_inc(T.sem.st, 16)
    g.wait_ge(T.sem.st, 16 * len(groups))
